import numpy as np
import ml_dtypes


def mxq(x, axis, fmt="e4m3"):
    dtype, down = {"e4m3": (ml_dtypes.float8_e4m3fn, 7), "e5m2": (ml_dtypes.float8_e5m2, 14)}[fmt]
    v = np.moveaxis(np.asarray(x, np.float32).astype(ml_dtypes.bfloat16).astype(np.float64), axis, -1)
    blocks = v.reshape(v.shape[:-1] + (-1, 32))
    amax = np.abs(blocks).max(-1, keepdims=True)
    byte = np.maximum(np.where(amax > 0, np.frexp(amax)[1] - 1 + 127, 0) - down, 1)
    scale = np.exp2(byte - 127.0)
    codes = (blocks / scale).astype(np.float32).astype(dtype).astype(np.float64)
    return np.moveaxis((codes * scale).reshape(v.shape), -1, axis)


WIDE = False


def mx_kscale(k):
    if not WIDE:
        return np.ones(k)
    levels = np.array([30, -30])
    if k % 512:
        return np.exp2(np.random.permutation(np.resize(levels, k // 32))).repeat(32)
    a = np.empty((k // 512, 16))
    for p in range(k // 512):
        a[p, :8] = np.random.permutation(np.resize(levels, 8))
        for g in range(8):
            far = levels[np.abs(levels - a[p, g]) >= 10]
            a[p, g + 8] = far[np.random.randint(len(far))]
    return np.exp2(a.ravel()).repeat(32)


def f64(x):
    return np.asarray(x).astype(np.float64)


def striped(idx):
    return np.tile(np.asarray(idx).reshape(-1, 16).T, (8, 1)).astype(np.uint16)


def unstriped(offs):
    return offs[:16].T.reshape(-1).astype(np.int64)


E2M1 = np.array([0.0, 0.5, 1.0, 1.5, 2.0, 3.0, 4.0, 6.0, -0.0, -0.5, -1.0, -1.5, -2.0, -3.0, -4.0, -6.0])


def pack_weight(w, fmt):
    k, n = w.shape
    w = f64(np.asarray(w, np.float32).astype(ml_dtypes.bfloat16)).reshape(k // 32, 32, n)
    amax = np.abs(w).max(1)
    if fmt in ("e4m3", "e5m2"):
        byte = np.frexp(amax)[1] - 1 + 127 - (7 if fmt == "e4m3" else 14)
    else:
        mant, ex = np.frexp(amax / 6.0)
        byte = np.where(mant > 0.5, ex, ex - 1) + 127
    byte = np.clip(np.where(amax > 0, byte, 1), 1, 254)
    scaled = (w * np.exp2(127.0 - byte)[:, None, :]).reshape(k, n).astype(np.float32)
    by_word = np.ascontiguousarray(scaled.reshape(k // 512, 128, 4, n).transpose(0, 1, 3, 2))
    if fmt in ("e4m3", "e5m2"):
        words = by_word.astype(ml_dtypes.float8_e4m3fn if fmt == "e4m3" else ml_dtypes.float8_e5m2).view(np.uint8)
    else:
        c = by_word.astype(ml_dtypes.float4_e2m1fn).view(np.uint8) & 0xF
        words = (c[..., 0::2] | (c[..., 1::2] << 4)).reshape(k // 512, 128, 2 * n)
    return np.ascontiguousarray(words), np.ascontiguousarray(byte.astype(np.uint8).reshape(k // 512, 16, n))


def unpack_weight(words, scales, fmt):
    g, _, n = scales.shape
    words = np.ascontiguousarray(words).reshape(g, 128, n, -1)
    if fmt in ("e4m3", "e5m2"):
        vals = words.view(ml_dtypes.float8_e4m3fn if fmt == "e4m3" else ml_dtypes.float8_e5m2).astype(np.float64)
    else:
        nib = np.empty((g, 128, n, 4), np.uint8)
        nib[..., 0::2] = words & 0xF
        nib[..., 1::2] = words >> 4
        vals = E2M1[nib]
    vals = vals * np.repeat(np.exp2(scales.astype(np.float64) - 127.0), 8, axis=1)[..., None]
    return vals.transpose(0, 1, 3, 2).reshape(g * 512, n)


K, T, J, I, R, V, G = 512, 512, 256, 256, 512, 512, 32


def setup_inputs():
    n = np.random.standard_normal
    idx = np.random.permutation(T)[:J]
    idx2 = np.random.permutation(V)[:J]
    idx3 = np.random.permutation(T)[:I]
    fk = mx_kscale(K)
    fr = mx_kscale(R)
    xtp = pack_weight(n((K, T)) / fk[:, None], "e5m2")
    wap = pack_weight(n((K, R)) * 0.5 / np.sqrt(K) * fk[:, None] * fr, "e2m1")
    wbp = pack_weight(n((K, R)) * 1 / np.sqrt(K) * fk[:, None] / fr, "e2m1")
    return {
        "xt_words": xtp[0],
        "xt_scales": xtp[1],
        "wa_words": wap[0],
        "wa_scales": wap[1],
        "tb": (n((R, V)) * 0.5 * fr[:, None]).astype(np.float32),
        "wb_words": wbp[0],
        "wb_scales": wbp[1],
        "tg": (np.random.uniform(-10.0, 20.0, (J, 1))).astype(np.float32),
        "cw1": (np.random.uniform(0.5, 2.0, (1, I))).astype(np.float32),
        "offs": striped(idx),
        "offs2": striped(idx2),
        "offs3": striped(idx3),
    }


def reference(xt_words, xt_scales, wa_words, wa_scales, tb, wb_words, wb_scales, tg, cw1, offs, offs2, offs3):
    idx = unstriped(offs)
    idx2 = unstriped(offs2)
    idx3 = unstriped(offs3)
    xtu = unpack_weight(xt_words, xt_scales, "e5m2")
    wau = unpack_weight(wa_words, wa_scales, "e2m1")
    wbu = unpack_weight(wb_words, wb_scales, "e2m1")
    xtidxg = xtu[:, idx]
    za = wau.T @ xtidxg
    ha = np.maximum(za - f64(tb)[:, idx2], 0.0)
    xtidx3g = xtu[:, idx3]
    zb = wbu.T @ xtidx3g
    mb1 = zb.reshape(R, G, I // G).mean(axis=2)
    mb2 = np.repeat(mb1, I // G, axis=1)
    hb = zb - mb2
    haq = mxq(ha, 0, "e5m2")
    hbq = mxq(hb, 0, "e5m2")
    a0 = haq.T @ hbq
    y = 0.04 * np.maximum(a0 - f64(tg), 0.0) * f64(cw1)
    return y

@@ -1,0 +1,202 @@
+from contextlib import ExitStack
+
+import concourse.mybir as mybir
+from concourse.masks import make_identity
+
+K, T, J, I, R, V = 512, 512, 256, 256, 512, 512
+FLOPS = 2 * K * R * J + 2 * K * R * I + 2 * R * J * I
+
+F32 = mybir.dt.float32
+BF16 = mybir.dt.bfloat16
+I32 = mybir.dt.int32
+U32 = mybir.dt.uint32
+U16 = mybir.dt.uint16
+U8 = mybir.dt.uint8
+E5M2X4 = mybir.dt.float8_e5m2_x4
+E2M1X4 = mybir.dt.float4_e2m1fn_x4
+ALU = mybir.AluOpType
+ACT = mybir.ActivationFunctionType
+
+P = 128
+PACK = 4
+HALF = 128
+BUNDLE = 8
+
+
+def tile_list_meet_overtable_levelled_hinge_kernel(
+    tc, xt_words, xt_scales, wa_words, wa_scales, tb, wb_words, wb_scales, tg, cw1, offs, offs2, offs3, out
+):
+    nc = tc.nc
+    with ExitStack() as ctx:
+        lists = ctx.enter_context(tc.tile_pool(name="lists", bufs=1))
+        sb = ctx.enter_context(tc.tile_pool(name="sb", bufs=1))
+        ps = ctx.enter_context(tc.psum_pool(name="ps", bufs=1))
+
+        def tile(name, shape, dtype):
+            return sb.tile(shape, dtype, name=name, align_bytes=64)
+
+        def load_scale_rows(queues, plane, scales):
+            rows = scales[0].bitcast(I32)
+            for quad in range(4):
+                queues[quad].dma_start(
+                    out=plane[32 * quad : 32 * quad + 4, :], in_=rows[4 * quad : 4 * quad + 4, :]
+                )
+
+        idx = lists.tile([P, J // 16], U16, name="idx")
+        idx2 = lists.tile([P, J // 16], U16, name="idx2")
+        idx3 = lists.tile([P, I // 16], U16, name="idx3")
+
+        x_words = tile("x_words", [P, T], I32)
+        x_plane = tile("x_plane", [P, T // 4], I32)
+        wa_raw = tile("wa_raw", [P, R // 2], I32)
+        wb_raw = tile("wb_raw", [P, R // 2], I32)
+        wa_plane = tile("wa_plane", [P, R // 4], I32)
+        wb_plane = tile("wb_plane", [P, R // 4], I32)
+        table = [tile(f"table{t}", [P, V], F32) for t in range(PACK)]
+        tg_col = tile("tg_col", [P, 2], F32)
+        cw_col = tile("cw_col", [P, 2], F32)
+
+        nc.vector.memset(x_plane[:], 0)
+        nc.vector.memset(wb_plane[:], 0)
+        nc.vector.memset(wa_plane[:], 0)
+
+        tb_dealt = tb.rearrange("(q t s) v -> t q s v", t=PACK, s=8)
+        nc.scalar.dma_start(out=x_words[:], in_=xt_words[0].rearrange("p c r -> p (c r)").bitcast(I32))
+        nc.sync.dma_start(out=idx3[:], in_=offs3)
+        load_scale_rows([nc.sync, nc.scalar, nc.sync, nc.scalar], x_plane, xt_scales)
+        nc.sync.dma_start(out=idx[:], in_=offs)
+        with nc.allow_non_contiguous_dma(reason="one value to a partition"):
+            nc.scalar.dma_start(out=tg_col[:], in_=tg.rearrange("(h p) o -> p (h o)", p=P))
+        for t in range(2):
+            nc.gpsimd.dma_start(out=table[t][:], in_=tb_dealt[t])
+        nc.sync.dma_start(out=wb_raw[:], in_=wb_words[0].bitcast(I32))
+        load_scale_rows([nc.sync] * 4, wb_plane, wb_scales)
+        nc.sync.dma_start(out=wa_raw[:], in_=wa_words[0].bitcast(I32))
+        nc.sync.dma_start(out=idx2[:], in_=offs2)
+        nc.sync.dma_start(out=table[2][:], in_=tb_dealt[2])
+        load_scale_rows([nc.sync] * 4, wa_plane, wa_scales)
+        nc.sync.dma_start(out=table[3][:], in_=tb_dealt[3])
+        with nc.allow_non_contiguous_dma(reason="one value to a partition"):
+            nc.sync.dma_start(out=cw_col[:], in_=cw1.rearrange("o (h p) -> p (o h)", p=P))
+
+        ident = tile("ident", [P, P], F32)
+        make_identity(nc, ident[:])
+        neg_tg = tile("neg_tg", [P, 2], F32)
+        nc.scalar.activation(neg_tg[:], tg_col[:], ACT.Copy, scale=-0.04)
+
+        def gather_tokens(name, offsets):
+            words = tile(name + "_words", [P, J], U32)
+            plane = tile(name + "_plane", [P, J], U8)
+            nc.vector.tensor_copy(plane[:], x_plane[:].bitcast(U8).indirect(offsets[:]))
+            nc.vector.tensor_copy(words[:], x_words[:].bitcast(U32).indirect(offsets[:]))
+            return words, plane
+
+        def deal_weight(name, raw, raw_plane):
+            words = tile(name + "_words", [P, R // 2], I32)
+            plane = tile(name + "_dealt", [P, R // 4], I32)
+            nc.vector.tensor_copy(
+                words[:].rearrange("p (t q w) -> p t q w", t=PACK, w=4),
+                raw[:].rearrange("p (q t w) -> p t q w", t=PACK, w=4),
+            )
+            nc.vector.tensor_copy(
+                plane[:].rearrange("p (t q w) -> p t q w", t=PACK, w=2),
+                raw_plane[:].rearrange("p (q t w) -> p t q w", t=PACK, w=2),
+            )
+            return words, plane
+
+        def first_stage(name, weight, tokens):
+            w_words, w_plane = weight
+            t_words, t_plane = tokens
+            banks = []
+            for h in range(2):
+                bank = ps.tile([P, PACK, HALF], F32, name=f"{name}{h}")
+                cols = slice(HALF * h, HALF * (h + 1))
+                for t in range(PACK):
+                    nc.tensor.matmul_mx(
+                        out=bank[:, t, :],
+                        lhsT=w_words[:].bitcast(U8)[:, 2 * P * t : 2 * P * (t + 1)].bitcast(E2M1X4),
+                        lhsT_scale=w_plane[:].bitcast(U8)[:, P * t : P * (t + 1)],
+                        rhs=t_words[:, cols].bitcast(E5M2X4),
+                        rhs_scale=t_plane[:, cols],
+                        start=True,
+                        stop=True,
+                    )
+                banks.append(bank)
+            return banks
+
+        tokens_b = gather_tokens("xb", idx3)
+        weight_b = deal_weight("wb", wb_raw, wb_plane)
+        zb = first_stage("zb", weight_b, tokens_b)
+        tokens_a = gather_tokens("xa", idx)
+        weight_a = deal_weight("wa", wa_raw, wa_plane)
+        za = first_stage("za", weight_a, tokens_a)
+
+        picked = tile("picked", [P, PACK, J], F32)
+        for t in range(PACK):
+            nc.scalar.activation(picked[:, t, :], table[t][:].indirect(idx2[:]), ACT.Copy)
+
+        cw_rows = ps.tile([P, I], F32, name="cw_rows")
+        for h in range(2):
+            nc.tensor.transpose(
+                cw_rows[:, HALF * h : HALF * (h + 1)], cw_col[:, h : h + 1].to_broadcast([P, P]), ident[:]
+            )
+
+        groups = HALF // BUNDLE
+        sums = tile("sums", [P, 2, groups, PACK], F32)
+        means = tile("means", [P, 2, groups, PACK], F32)
+        for h in range(2):
+            nc.vector.tensor_reduce(
+                sums[:, h], zb[h][:].rearrange("p t (g e) -> p g t e", e=BUNDLE), mybir.AxisListType.X, ALU.add
+            )
+        nc.gpsimd.tensor_scalar(
+            means[:].rearrange("p h g t -> p (h g t)"),
+            sums[:].rearrange("p h g t -> p (h g t)"),
+            1.0 / BUNDLE,
+            0.0,
+            ALU.mult,
+            ALU.add,
+        )
+
+        ha = tile("ha", [P, J * PACK], BF16)
+        for h in range(2):
+            diff = tile(f"diff{h}", [P, PACK, HALF], F32)
+            nc.vector.tensor_tensor(diff[:], za[h][:], picked[:, :, HALF * h : HALF * (h + 1)], ALU.subtract)
+            nc.scalar.activation(
+                ha[:, 512 * h : 512 * (h + 1)].rearrange("p (j t) -> p j t", t=PACK),
+                diff[:].rearrange("p t j -> p j t"),
+                ACT.Relu,
+            )
+
+        hb = tile("hb", [P, I * PACK], BF16)
+        for h in range(2):
+            nc.vector.tensor_tensor(
+                hb[:, 512 * h : 512 * (h + 1)].rearrange("p (g e t) -> p g e t", e=BUNDLE, t=PACK),
+                zb[h][:].rearrange("p t (g e) -> p g e t", e=BUNDLE),
+                means[:, h].unsqueeze(2).broadcast_to([P, groups, BUNDLE, PACK]),
+                ALU.subtract,
+            )
+
+        ha_words = tile("ha_words", [P, J], U32)
+        ha_plane = tile("ha_plane", [P, J], U8)
+        hb_words = tile("hb_words", [P, I], U32)
+        hb_plane = tile("hb_plane", [P, I], U8)
+        nc.vector.quantize_mx(out=ha_words[:].bitcast(E5M2X4), scales=ha_plane[:], in_=ha[:])
+        nc.vector.quantize_mx(out=hb_words[:].bitcast(E5M2X4), scales=hb_plane[:], in_=hb[:])
+
+        for h in range(2):
+            rows = slice(HALF * h, HALF * (h + 1))
+            score = ps.tile([P, I], F32, name=f"score{h}")
+            nc.tensor.matmul_mx(
+                out=score[:],
+                lhsT=ha_words[:, rows].bitcast(E5M2X4),
+                lhsT_scale=ha_plane[:, rows],
+                rhs=hb_words[:].bitcast(E5M2X4),
+                rhs_scale=hb_plane[:],
+                start=True,
+                stop=True,
+            )
+            hinge = tile(f"hinge{h}", [P, I], F32)
+            nc.scalar.activation(hinge[:], score[:], ACT.Relu, bias=neg_tg[:, h : h + 1], scale=0.04)
+            result = tile(f"result{h}", [P, I], F32)
+            nc.vector.tensor_tensor(result[:], hinge[:], cw_rows[:], ALU.mult)
+            (nc.sync if h == 0 else nc.scalar).dma_start(out=out[rows, :], in_=result[:])

@@ -35,12 +35,12 @@ def tile_list_meet_overtable_levelled_hinge_kernel(
         def tile(name, shape, dtype):
             return sb.tile(shape, dtype, name=name, align_bytes=64)
 
-        def load_scale_rows(queues, plane, scales):
-            rows = scales[0].bitcast(I32)
-            for quad in range(4):
-                queues[quad].dma_start(
-                    out=plane[32 * quad : 32 * quad + 4, :], in_=rows[4 * quad : 4 * quad + 4, :]
-                )
+        def load_first_scale_rows(queue, plane, scales):
+            queue.dma_start(out=plane[0:2, :], in_=scales[0].bitcast(I32)[0:2, :])
+
+        def load_other_scale_rows(queue, plane, scales):
+            rows = scales[0].bitcast(I32)[2:16, :]
+            queue.dma_start(out=plane[2:P, :], in_=rows.unsqueeze(0).broadcast_to([9, 14, rows.shape[1]]))
 
         idx = lists.tile([P, J // 16], U16, name="idx")
         idx2 = lists.tile([P, J // 16], U16, name="idx2")
@@ -56,39 +56,34 @@ def tile_list_meet_overtable_levelled_hinge_kernel(
         tg_col = tile("tg_col", [P, 2], F32)
         cw_col = tile("cw_col", [P, 2], F32)
 
-        nc.vector.memset(x_plane[:], 0)
-        nc.vector.memset(wb_plane[:], 0)
-        nc.vector.memset(wa_plane[:], 0)
-
         tb_dealt = tb.rearrange("(q t s) v -> t q s v", t=PACK, s=8)
-        nc.scalar.dma_start(out=x_words[:], in_=xt_words[0].rearrange("p c r -> p (c r)").bitcast(I32))
+        load_other_scale_rows(nc.scalar, x_plane, xt_scales)
+        load_other_scale_rows(nc.gpsimd, wb_plane, wb_scales)
+        load_other_scale_rows(nc.gpsimd, wa_plane, wa_scales)
+        nc.sync.dma_start(out=x_words[:], in_=xt_words[0].rearrange("p c r -> p (c r)").bitcast(I32))
         nc.sync.dma_start(out=idx3[:], in_=offs3)
-        load_scale_rows([nc.sync, nc.scalar, nc.sync, nc.scalar], x_plane, xt_scales)
-        nc.sync.dma_start(out=idx[:], in_=offs)
-        with nc.allow_non_contiguous_dma(reason="one value to a partition"):
-            nc.scalar.dma_start(out=tg_col[:], in_=tg.rearrange("(h p) o -> p (h o)", p=P))
-        for t in range(2):
-            nc.gpsimd.dma_start(out=table[t][:], in_=tb_dealt[t])
+        load_first_scale_rows(nc.sync, x_plane, xt_scales)
         nc.sync.dma_start(out=wb_raw[:], in_=wb_words[0].bitcast(I32))
-        load_scale_rows([nc.sync] * 4, wb_plane, wb_scales)
+        load_first_scale_rows(nc.sync, wb_plane, wb_scales)
+        nc.sync.dma_start(out=idx[:], in_=offs)
         nc.sync.dma_start(out=wa_raw[:], in_=wa_words[0].bitcast(I32))
+        load_first_scale_rows(nc.sync, wa_plane, wa_scales)
         nc.sync.dma_start(out=idx2[:], in_=offs2)
-        nc.sync.dma_start(out=table[2][:], in_=tb_dealt[2])
-        load_scale_rows([nc.sync] * 4, wa_plane, wa_scales)
-        nc.sync.dma_start(out=table[3][:], in_=tb_dealt[3])
+        with nc.allow_non_contiguous_dma(reason="one value to a partition"):
+            nc.sync.dma_start(out=tg_col[:], in_=tg.rearrange("(h p) o -> p (h o)", p=P))
+        for t in range(PACK):
+            nc.sync.dma_start(out=table[t][:], in_=tb_dealt[t])
         with nc.allow_non_contiguous_dma(reason="one value to a partition"):
             nc.sync.dma_start(out=cw_col[:], in_=cw1.rearrange("o (h p) -> p (o h)", p=P))
 
-        ident = tile("ident", [P, P], F32)
-        make_identity(nc, ident[:])
         neg_tg = tile("neg_tg", [P, 2], F32)
         nc.scalar.activation(neg_tg[:], tg_col[:], ACT.Copy, scale=-0.04)
 
         def gather_tokens(name, offsets):
             words = tile(name + "_words", [P, J], U32)
             plane = tile(name + "_plane", [P, J], U8)
-            nc.vector.tensor_copy(plane[:], x_plane[:].bitcast(U8).indirect(offsets[:]))
             nc.vector.tensor_copy(words[:], x_words[:].bitcast(U32).indirect(offsets[:]))
+            nc.vector.tensor_copy(plane[:], x_plane[:].bitcast(U8).indirect(offsets[:]))
             return words, plane
 
         def deal_weight(name, raw, raw_plane):
@@ -135,6 +130,8 @@ def tile_list_meet_overtable_levelled_hinge_kernel(
         for t in range(PACK):
             nc.scalar.activation(picked[:, t, :], table[t][:].indirect(idx2[:]), ACT.Copy)
 
+        ident = sb.tile([P, P], F32, name="ident", tag="wa_raw", align_bytes=64)
+        make_identity(nc, ident[:])
         cw_rows = ps.tile([P, I], F32, name="cw_rows")
         for h in range(2):
             nc.tensor.transpose(
@@ -142,54 +139,52 @@ def tile_list_meet_overtable_levelled_hinge_kernel(
             )
 
         groups = HALF // BUNDLE
-        sums = tile("sums", [P, 2, groups, PACK], F32)
-        means = tile("means", [P, 2, groups, PACK], F32)
+        means = []
         for h in range(2):
+            sums = tile(f"sums{h}", [P, groups * PACK], F32)
+            mean = tile(f"mean{h}", [P, groups * PACK], F32)
             nc.vector.tensor_reduce(
-                sums[:, h], zb[h][:].rearrange("p t (g e) -> p g t e", e=BUNDLE), mybir.AxisListType.X, ALU.add
+                sums[:].rearrange("p (g t) -> p g t", t=PACK),
+                zb[h][:].rearrange("p t (g e) -> p g t e", e=BUNDLE),
+                mybir.AxisListType.X,
+                ALU.add,
             )
-        nc.gpsimd.tensor_scalar(
-            means[:].rearrange("p h g t -> p (h g t)"),
-            sums[:].rearrange("p h g t -> p (h g t)"),
-            1.0 / BUNDLE,
-            0.0,
-            ALU.mult,
-            ALU.add,
-        )
-
-        ha = tile("ha", [P, J * PACK], BF16)
-        for h in range(2):
-            diff = tile(f"diff{h}", [P, PACK, HALF], F32)
-            nc.vector.tensor_tensor(diff[:], za[h][:], picked[:, :, HALF * h : HALF * (h + 1)], ALU.subtract)
-            nc.scalar.activation(
-                ha[:, 512 * h : 512 * (h + 1)].rearrange("p (j t) -> p j t", t=PACK),
-                diff[:].rearrange("p t j -> p j t"),
-                ACT.Relu,
-            )
+            nc.gpsimd.tensor_scalar(mean[:], sums[:], 1.0 / BUNDLE, 0.0, ALU.mult, ALU.add)
+            means.append(mean)
 
         hb = tile("hb", [P, I * PACK], BF16)
         for h in range(2):
             nc.vector.tensor_tensor(
                 hb[:, 512 * h : 512 * (h + 1)].rearrange("p (g e t) -> p g e t", e=BUNDLE, t=PACK),
                 zb[h][:].rearrange("p t (g e) -> p g e t", e=BUNDLE),
-                means[:, h].unsqueeze(2).broadcast_to([P, groups, BUNDLE, PACK]),
+                means[h][:].rearrange("p (g t) -> p g t", t=PACK).unsqueeze(2).broadcast_to([P, groups, BUNDLE, PACK]),
                 ALU.subtract,
             )
 
-        ha_words = tile("ha_words", [P, J], U32)
-        ha_plane = tile("ha_plane", [P, J], U8)
+        ha = []
+        for h in range(2):
+            diff = tile(f"diff{h}", [P, PACK, HALF], F32)
+            nc.vector.tensor_tensor(diff[:], za[h][:], picked[:, :, HALF * h : HALF * (h + 1)], ALU.subtract)
+            ha.append(tile(f"ha{h}", [P, HALF * PACK], BF16))
+            nc.scalar.activation(
+                ha[h][:].rearrange("p (j t) -> p j t", t=PACK), diff[:].rearrange("p t j -> p j t"), ACT.Relu
+            )
+
         hb_words = tile("hb_words", [P, I], U32)
         hb_plane = tile("hb_plane", [P, I], U8)
-        nc.vector.quantize_mx(out=ha_words[:].bitcast(E5M2X4), scales=ha_plane[:], in_=ha[:])
         nc.vector.quantize_mx(out=hb_words[:].bitcast(E5M2X4), scales=hb_plane[:], in_=hb[:])
+        ha_words = [tile(f"ha_words{h}", [P, HALF], U32) for h in range(2)]
+        ha_plane = [tile(f"ha_plane{h}", [P, HALF], U8) for h in range(2)]
+        for h in range(2):
+            nc.vector.quantize_mx(out=ha_words[h][:].bitcast(E5M2X4), scales=ha_plane[h][:], in_=ha[h][:])
 
         for h in range(2):
             rows = slice(HALF * h, HALF * (h + 1))
             score = ps.tile([P, I], F32, name=f"score{h}")
             nc.tensor.matmul_mx(
                 out=score[:],
-                lhsT=ha_words[:, rows].bitcast(E5M2X4),
-                lhsT_scale=ha_plane[:, rows],
+                lhsT=ha_words[h][:].bitcast(E5M2X4),
+                lhsT_scale=ha_plane[h][:],
                 rhs=hb_words[:].bitcast(E5M2X4),
                 rhs_scale=hb_plane[:],
                 start=True,

@@ -1,7 +1,6 @@
 from contextlib import ExitStack
 
 import concourse.mybir as mybir
-from concourse.masks import make_identity
 
 K, T, J, I, R, V = 512, 512, 256, 256, 512, 512
 FLOPS = 2 * K * R * J + 2 * K * R * I + 2 * R * J * I
@@ -57,45 +56,48 @@ def tile_list_meet_overtable_levelled_hinge_kernel(
         cw_col = tile("cw_col", [P, 2], F32)
 
         tb_dealt = tb.rearrange("(q t s) v -> t q s v", t=PACK, s=8)
-        load_other_scale_rows(nc.scalar, x_plane, xt_scales)
         load_other_scale_rows(nc.gpsimd, wb_plane, wb_scales)
         load_other_scale_rows(nc.gpsimd, wa_plane, wa_scales)
-        nc.sync.dma_start(out=x_words[:], in_=xt_words[0].rearrange("p c r -> p (c r)").bitcast(I32))
         nc.sync.dma_start(out=idx3[:], in_=offs3)
+        nc.scalar.dma_start(out=x_words[:], in_=xt_words[0].rearrange("p c r -> p (c r)").bitcast(I32))
         load_first_scale_rows(nc.sync, x_plane, xt_scales)
-        nc.sync.dma_start(out=wb_raw[:], in_=wb_words[0].bitcast(I32))
-        load_first_scale_rows(nc.sync, wb_plane, wb_scales)
+        nc.scalar.dma_start(out=wb_raw[:], in_=wb_words[0].bitcast(I32))
         nc.sync.dma_start(out=idx[:], in_=offs)
+        load_other_scale_rows(nc.scalar, x_plane, xt_scales)
+        load_first_scale_rows(nc.sync, wb_plane, wb_scales)
+        nc.sync.dma_start(out=table[0][:], in_=tb_dealt[0])
+        nc.sync.dma_start(out=idx2[:], in_=offs2)
+        nc.sync.dma_start(out=table[1][:], in_=tb_dealt[1])
+        nc.sync.dma_start(out=table[2][:], in_=tb_dealt[2])
         nc.sync.dma_start(out=wa_raw[:], in_=wa_words[0].bitcast(I32))
         load_first_scale_rows(nc.sync, wa_plane, wa_scales)
-        nc.sync.dma_start(out=idx2[:], in_=offs2)
+        nc.sync.dma_start(out=table[3][:], in_=tb_dealt[3])
         with nc.allow_non_contiguous_dma(reason="one value to a partition"):
             nc.sync.dma_start(out=tg_col[:], in_=tg.rearrange("(h p) o -> p (h o)", p=P))
-        for t in range(PACK):
-            nc.sync.dma_start(out=table[t][:], in_=tb_dealt[t])
-        with nc.allow_non_contiguous_dma(reason="one value to a partition"):
             nc.sync.dma_start(out=cw_col[:], in_=cw1.rearrange("o (h p) -> p (o h)", p=P))
 
-        neg_tg = tile("neg_tg", [P, 2], F32)
-        nc.scalar.activation(neg_tg[:], tg_col[:], ACT.Copy, scale=-0.04)
+        off_diagonal = tile("off_diagonal", [P, P], F32)
+        distance = tile("distance", [P, P], F32)
+        ident = tile("ident", [P, P], F32)
+        nc.gpsimd.iota(off_diagonal[:], [[1, P]], base=0, channel_multiplier=-1, allow_small_or_imprecise_dtypes=True)
+        nc.scalar.activation(distance[:], off_diagonal[:], ACT.Abs)
+        nc.scalar.activation(ident[:], distance[:], ACT.Relu, bias=1.0, scale=-1.0)
 
-        def gather_tokens(name, offsets):
-            words = tile(name + "_words", [P, J], U32)
-            plane = tile(name + "_plane", [P, J], U8)
-            nc.vector.tensor_copy(words[:], x_words[:].bitcast(U32).indirect(offsets[:]))
-            nc.vector.tensor_copy(plane[:], x_plane[:].bitcast(U8).indirect(offsets[:]))
-            return words, plane
+        def gather(name, window, offsets):
+            picked_columns = tile(name, [P, J], window.dtype)
+            nc.vector.tensor_copy(picked_columns[:], window.indirect(offsets[:]))
+            return picked_columns
 
         def deal_weight(name, raw, raw_plane):
-            words = tile(name + "_words", [P, R // 2], I32)
-            plane = tile(name + "_dealt", [P, R // 4], I32)
-            nc.vector.tensor_copy(
+            words = tile(name + "_words", [P, R // 2], U32)
+            plane = tile(name + "_dealt", [P, R // 4], U32)
+            nc.scalar.copy(
                 words[:].rearrange("p (t q w) -> p t q w", t=PACK, w=4),
-                raw[:].rearrange("p (q t w) -> p t q w", t=PACK, w=4),
+                raw[:].bitcast(U32).rearrange("p (q t w) -> p t q w", t=PACK, w=4),
             )
-            nc.vector.tensor_copy(
+            nc.scalar.copy(
                 plane[:].rearrange("p (t q w) -> p t q w", t=PACK, w=2),
-                raw_plane[:].rearrange("p (q t w) -> p t q w", t=PACK, w=2),
+                raw_plane[:].bitcast(U32).rearrange("p (q t w) -> p t q w", t=PACK, w=2),
             )
             return words, plane
 
@@ -119,19 +121,23 @@ def tile_list_meet_overtable_levelled_hinge_kernel(
                 banks.append(bank)
             return banks
 
-        tokens_b = gather_tokens("xb", idx3)
-        weight_b = deal_weight("wb", wb_raw, wb_plane)
-        zb = first_stage("zb", weight_b, tokens_b)
-        tokens_a = gather_tokens("xa", idx)
-        weight_a = deal_weight("wa", wa_raw, wa_plane)
-        za = first_stage("za", weight_a, tokens_a)
+        xb_words = gather("xb_words", x_words[:].bitcast(U32), idx3)
+        xa_words = gather("xa_words", x_words[:].bitcast(U32), idx)
+        xb_plane = gather("xb_plane", x_plane[:].bitcast(U8), idx3)
+        xa_plane = gather("xa_plane", x_plane[:].bitcast(U8), idx)
 
         picked = tile("picked", [P, PACK, J], F32)
-        for t in range(PACK):
+
+        def pick_table(t):
             nc.scalar.activation(picked[:, t, :], table[t][:].indirect(idx2[:]), ACT.Copy)
 
-        ident = sb.tile([P, P], F32, name="ident", tag="wa_raw", align_bytes=64)
-        make_identity(nc, ident[:])
+        zb = first_stage("zb", deal_weight("wb", wb_raw, wb_plane), (xb_words, xb_plane))
+        pick_table(0)
+        pick_table(1)
+        pick_table(2)
+        za = first_stage("za", deal_weight("wa", wa_raw, wa_plane), (xa_words, xa_plane))
+        pick_table(3)
+
         cw_rows = ps.tile([P, I], F32, name="cw_rows")
         for h in range(2):
             nc.tensor.transpose(
@@ -152,6 +158,9 @@ def tile_list_meet_overtable_levelled_hinge_kernel(
             nc.gpsimd.tensor_scalar(mean[:], sums[:], 1.0 / BUNDLE, 0.0, ALU.mult, ALU.add)
             means.append(mean)
 
+        neg_tg = sb.tile([P, 2], F32, name="neg_tg", tag="sums1", align_bytes=64)
+        nc.gpsimd.tensor_scalar(neg_tg[:], tg_col[:], -0.04, 0.0, ALU.mult, ALU.add)
+
         hb = tile("hb", [P, I * PACK], BF16)
         for h in range(2):
             nc.vector.tensor_tensor(
@@ -162,12 +171,15 @@ def tile_list_meet_overtable_levelled_hinge_kernel(
             )
 
         ha = []
+        diffs = sb.tile([P, 2, PACK, HALF], F32, name="diffs", tag="mean1", align_bytes=64)
         for h in range(2):
-            diff = tile(f"diff{h}", [P, PACK, HALF], F32)
-            nc.vector.tensor_tensor(diff[:], za[h][:], picked[:, :, HALF * h : HALF * (h + 1)], ALU.subtract)
+            diff = diffs[:, h]
+            nc.vector.tensor_tensor(diff, za[h][:], picked[:, :, HALF * h : HALF * (h + 1)], ALU.subtract)
             ha.append(tile(f"ha{h}", [P, HALF * PACK], BF16))
             nc.scalar.activation(
-                ha[h][:].rearrange("p (j t) -> p j t", t=PACK), diff[:].rearrange("p t j -> p j t"), ACT.Relu
+                ha[h][:].rearrange("p (c i t) -> p c t i", i=4, t=PACK),
+                diff.rearrange("p t (c i) -> p c t i", i=4),
+                ACT.Relu,
             )
 
         hb_words = tile("hb_words", [P, I], U32)

@@ -61,9 +61,9 @@ def tile_list_meet_overtable_levelled_hinge_kernel(
         nc.sync.dma_start(out=idx3[:], in_=offs3)
         nc.scalar.dma_start(out=x_words[:], in_=xt_words[0].rearrange("p c r -> p (c r)").bitcast(I32))
         load_first_scale_rows(nc.sync, x_plane, xt_scales)
-        nc.scalar.dma_start(out=wb_raw[:], in_=wb_words[0].bitcast(I32))
-        nc.sync.dma_start(out=idx[:], in_=offs)
         load_other_scale_rows(nc.scalar, x_plane, xt_scales)
+        nc.sync.dma_start(out=wb_raw[:], in_=wb_words[0].bitcast(I32))
+        nc.sync.dma_start(out=idx[:], in_=offs)
         load_first_scale_rows(nc.sync, wb_plane, wb_scales)
         nc.sync.dma_start(out=table[0][:], in_=tb_dealt[0])
         nc.sync.dma_start(out=idx2[:], in_=offs2)
@@ -88,8 +88,8 @@ def tile_list_meet_overtable_levelled_hinge_kernel(
             nc.vector.tensor_copy(picked_columns[:], window.indirect(offsets[:]))
             return picked_columns
 
-        def deal_weight(name, raw, raw_plane):
-            words = tile(name + "_words", [P, R // 2], U32)
+        def deal_weight(name, raw, raw_plane, tag):
+            words = sb.tile([P, R // 2], U32, name=name + "_words", tag=tag, align_bytes=64)
             plane = tile(name + "_dealt", [P, R // 4], U32)
             nc.scalar.copy(
                 words[:].rearrange("p (t q w) -> p t q w", t=PACK, w=4),
@@ -126,22 +126,19 @@ def tile_list_meet_overtable_levelled_hinge_kernel(
         xb_plane = gather("xb_plane", x_plane[:].bitcast(U8), idx3)
         xa_plane = gather("xa_plane", x_plane[:].bitcast(U8), idx)
 
-        picked = tile("picked", [P, PACK, J], F32)
 
         def pick_table(t):
             nc.scalar.activation(picked[:, t, :], table[t][:].indirect(idx2[:]), ACT.Copy)
 
-        zb = first_stage("zb", deal_weight("wb", wb_raw, wb_plane), (xb_words, xb_plane))
+        zb = first_stage("zb", deal_weight("wb", wb_raw, wb_plane, "wb_words"), (xb_words, xb_plane))
+        picked = sb.tile([P, PACK, J], F32, name="picked", tag="wb_plane", align_bytes=64)
         pick_table(0)
         pick_table(1)
         pick_table(2)
-        za = first_stage("za", deal_weight("wa", wa_raw, wa_plane), (xa_words, xa_plane))
-        pick_table(3)
-
-        cw_rows = ps.tile([P, I], F32, name="cw_rows")
+        za = first_stage("za", deal_weight("wa", wa_raw, wa_plane, "wb_raw"), (xa_words, xa_plane))
         for h in range(2):
-            nc.tensor.transpose(
-                cw_rows[:, HALF * h : HALF * (h + 1)], cw_col[:, h : h + 1].to_broadcast([P, P]), ident[:]
+            nc.scalar.activation(
+                picked[:, 3, HALF * h : HALF * (h + 1)], table[3][:].indirect(idx2[:, 8 * h : 8 * (h + 1)]), ACT.Copy
             )
 
         groups = HALF // BUNDLE
@@ -170,21 +167,30 @@ def tile_list_meet_overtable_levelled_hinge_kernel(
                 ALU.subtract,
             )
 
-        ha = []
-        diffs = sb.tile([P, 2, PACK, HALF], F32, name="diffs", tag="mean1", align_bytes=64)
+        cw_rows = ps.tile([P, I], F32, name="cw_rows", tag="zb0")
         for h in range(2):
-            diff = diffs[:, h]
-            nc.vector.tensor_tensor(diff, za[h][:], picked[:, :, HALF * h : HALF * (h + 1)], ALU.subtract)
-            ha.append(tile(f"ha{h}", [P, HALF * PACK], BF16))
-            nc.scalar.activation(
-                ha[h][:].rearrange("p (c i t) -> p c t i", i=4, t=PACK),
-                diff.rearrange("p t (c i) -> p c t i", i=4),
-                ACT.Relu,
+            nc.tensor.transpose(
+                cw_rows[:, HALF * h : HALF * (h + 1)], cw_col[:, h : h + 1].to_broadcast([P, P]), ident[:]
             )
 
+        diffs = sb.tile([P, 2, PACK, HALF], F32, name="diffs", tag="mean1", align_bytes=64)
+        ha = [tile(f"ha{h}", [P, HALF * PACK], BF16) for h in range(2)]
+
+        def interleaved(h, first, last):
+            return (
+                ha[h][:, PACK * first : PACK * last].rearrange("p (c i t) -> p c t i", i=4, t=PACK),
+                diffs[:, h, :, first:last].rearrange("p t (c i) -> p c t i", i=4),
+            )
+
+        for h in range(2):
+            nc.vector.tensor_tensor(diffs[:, h], za[h][:], picked[:, :, HALF * h : HALF * (h + 1)], ALU.subtract)
+        nc.scalar.activation(*interleaved(0, 0, HALF), ACT.Relu)
+        nc.scalar.activation(*interleaved(1, 0, HALF // 2), ACT.Relu)
         hb_words = tile("hb_words", [P, I], U32)
         hb_plane = tile("hb_plane", [P, I], U8)
         nc.vector.quantize_mx(out=hb_words[:].bitcast(E5M2X4), scales=hb_plane[:], in_=hb[:])
+        nc.vector.tensor_scalar_max(*interleaved(1, HALF // 2, HALF), 0.0)
+
         ha_words = [tile(f"ha_words{h}", [P, HALF], U32) for h in range(2)]
         ha_plane = [tile(f"ha_plane{h}", [P, HALF], U8) for h in range(2)]
         for h in range(2):

from contextlib import ExitStack

import concourse.mybir as mybir

K, T, J, I, R, V = 512, 512, 256, 256, 512, 512
FLOPS = 2 * K * R * J + 2 * K * R * I + 2 * R * J * I

F32 = mybir.dt.float32
BF16 = mybir.dt.bfloat16
I32 = mybir.dt.int32
U32 = mybir.dt.uint32
U16 = mybir.dt.uint16
U8 = mybir.dt.uint8
E5M2X4 = mybir.dt.float8_e5m2_x4
E2M1X4 = mybir.dt.float4_e2m1fn_x4
ALU = mybir.AluOpType
ACT = mybir.ActivationFunctionType

P = 128
PACK = 4
HALF = 128
BUNDLE = 8


def tile_list_meet_overtable_levelled_hinge_kernel(
    tc, xt_words, xt_scales, wa_words, wa_scales, tb, wb_words, wb_scales, tg, cw1, offs, offs2, offs3, out
):
    nc = tc.nc
    with ExitStack() as ctx:
        lists = ctx.enter_context(tc.tile_pool(name="lists", bufs=1))
        sb = ctx.enter_context(tc.tile_pool(name="sb", bufs=1))
        ps = ctx.enter_context(tc.psum_pool(name="ps", bufs=1))

        def tile(name, shape, dtype):
            return sb.tile(shape, dtype, name=name, align_bytes=64)

        def load_first_scale_rows(queue, plane, scales):
            queue.dma_start(out=plane[0:2, :], in_=scales[0].bitcast(I32)[0:2, :])

        def load_other_scale_rows(queue, plane, scales):
            rows = scales[0].bitcast(I32)[2:16, :]
            queue.dma_start(out=plane[2:P, :], in_=rows.unsqueeze(0).broadcast_to([9, 14, rows.shape[1]]))

        idx = lists.tile([P, J // 16], U16, name="idx")
        idx2 = lists.tile([P, J // 16], U16, name="idx2")
        idx3 = lists.tile([P, I // 16], U16, name="idx3")

        x_words = tile("x_words", [P, T], I32)
        x_plane = tile("x_plane", [P, T // 4], I32)
        wa_raw = tile("wa_raw", [P, R // 2], I32)
        wb_raw = tile("wb_raw", [P, R // 2], I32)
        wa_plane = tile("wa_plane", [P, R // 4], I32)
        wb_plane = tile("wb_plane", [P, R // 4], I32)
        table = [tile(f"table{t}", [P, V], F32) for t in range(PACK)]
        tg_col = tile("tg_col", [P, 2], F32)
        cw_col = tile("cw_col", [P, 2], F32)

        tb_dealt = tb.rearrange("(q t s) v -> t q s v", t=PACK, s=8)
        load_other_scale_rows(nc.gpsimd, wb_plane, wb_scales)
        load_other_scale_rows(nc.gpsimd, wa_plane, wa_scales)
        nc.sync.dma_start(out=idx3[:], in_=offs3)
        nc.scalar.dma_start(out=x_words[:], in_=xt_words[0].rearrange("p c r -> p (c r)").bitcast(I32))
        load_first_scale_rows(nc.sync, x_plane, xt_scales)
        load_other_scale_rows(nc.scalar, x_plane, xt_scales)
        nc.sync.dma_start(out=wb_raw[:], in_=wb_words[0].bitcast(I32))
        nc.sync.dma_start(out=idx[:], in_=offs)
        load_first_scale_rows(nc.sync, wb_plane, wb_scales)
        nc.sync.dma_start(out=table[0][:], in_=tb_dealt[0])
        nc.sync.dma_start(out=idx2[:], in_=offs2)
        nc.sync.dma_start(out=table[1][:], in_=tb_dealt[1])
        nc.sync.dma_start(out=table[2][:], in_=tb_dealt[2])
        nc.sync.dma_start(out=wa_raw[:], in_=wa_words[0].bitcast(I32))
        load_first_scale_rows(nc.sync, wa_plane, wa_scales)
        nc.sync.dma_start(out=table[3][:], in_=tb_dealt[3])
        with nc.allow_non_contiguous_dma(reason="one value to a partition"):
            nc.sync.dma_start(out=tg_col[:], in_=tg.rearrange("(h p) o -> p (h o)", p=P))
            nc.sync.dma_start(out=cw_col[:], in_=cw1.rearrange("o (h p) -> p (o h)", p=P))

        off_diagonal = tile("off_diagonal", [P, P], F32)
        distance = tile("distance", [P, P], F32)
        ident = tile("ident", [P, P], F32)
        nc.gpsimd.iota(off_diagonal[:], [[1, P]], base=0, channel_multiplier=-1, allow_small_or_imprecise_dtypes=True)
        nc.scalar.activation(distance[:], off_diagonal[:], ACT.Abs)
        nc.scalar.activation(ident[:], distance[:], ACT.Relu, bias=1.0, scale=-1.0)

        def gather(name, window, offsets):
            picked_columns = tile(name, [P, J], window.dtype)
            nc.vector.tensor_copy(picked_columns[:], window.indirect(offsets[:]))
            return picked_columns

        def deal_weight(name, raw, raw_plane, tag):
            words = sb.tile([P, R // 2], U32, name=name + "_words", tag=tag, align_bytes=64)
            plane = tile(name + "_dealt", [P, R // 4], U32)
            nc.scalar.copy(
                words[:].rearrange("p (t q w) -> p t q w", t=PACK, w=4),
                raw[:].bitcast(U32).rearrange("p (q t w) -> p t q w", t=PACK, w=4),
            )
            nc.scalar.copy(
                plane[:].rearrange("p (t q w) -> p t q w", t=PACK, w=2),
                raw_plane[:].bitcast(U32).rearrange("p (q t w) -> p t q w", t=PACK, w=2),
            )
            return words, plane

        def first_stage(name, weight, tokens):
            w_words, w_plane = weight
            t_words, t_plane = tokens
            banks = []
            for h in range(2):
                bank = ps.tile([P, PACK, HALF], F32, name=f"{name}{h}")
                cols = slice(HALF * h, HALF * (h + 1))
                for t in range(PACK):
                    nc.tensor.matmul_mx(
                        out=bank[:, t, :],
                        lhsT=w_words[:].bitcast(U8)[:, 2 * P * t : 2 * P * (t + 1)].bitcast(E2M1X4),
                        lhsT_scale=w_plane[:].bitcast(U8)[:, P * t : P * (t + 1)],
                        rhs=t_words[:, cols].bitcast(E5M2X4),
                        rhs_scale=t_plane[:, cols],
                        start=True,
                        stop=True,
                    )
                banks.append(bank)
            return banks

        xb_words = gather("xb_words", x_words[:].bitcast(U32), idx3)
        xa_words = gather("xa_words", x_words[:].bitcast(U32), idx)
        xb_plane = gather("xb_plane", x_plane[:].bitcast(U8), idx3)
        xa_plane = gather("xa_plane", x_plane[:].bitcast(U8), idx)


        def pick_table(t):
            nc.scalar.activation(picked[:, t, :], table[t][:].indirect(idx2[:]), ACT.Copy)

        zb = first_stage("zb", deal_weight("wb", wb_raw, wb_plane, "wb_words"), (xb_words, xb_plane))
        picked = sb.tile([P, PACK, J], F32, name="picked", tag="wb_plane", align_bytes=64)
        pick_table(0)
        pick_table(1)
        pick_table(2)
        za = first_stage("za", deal_weight("wa", wa_raw, wa_plane, "wb_raw"), (xa_words, xa_plane))
        for h in range(2):
            nc.scalar.activation(
                picked[:, 3, HALF * h : HALF * (h + 1)], table[3][:].indirect(idx2[:, 8 * h : 8 * (h + 1)]), ACT.Copy
            )

        groups = HALF // BUNDLE
        means = []
        for h in range(2):
            sums = tile(f"sums{h}", [P, groups * PACK], F32)
            mean = tile(f"mean{h}", [P, groups * PACK], F32)
            nc.vector.tensor_reduce(
                sums[:].rearrange("p (g t) -> p g t", t=PACK),
                zb[h][:].rearrange("p t (g e) -> p g t e", e=BUNDLE),
                mybir.AxisListType.X,
                ALU.add,
            )
            nc.gpsimd.tensor_scalar(mean[:], sums[:], 1.0 / BUNDLE, 0.0, ALU.mult, ALU.add)
            means.append(mean)

        neg_tg = sb.tile([P, 2], F32, name="neg_tg", tag="sums1", align_bytes=64)
        nc.gpsimd.tensor_scalar(neg_tg[:], tg_col[:], -0.04, 0.0, ALU.mult, ALU.add)

        hb = tile("hb", [P, I * PACK], BF16)
        for h in range(2):
            nc.vector.tensor_tensor(
                hb[:, 512 * h : 512 * (h + 1)].rearrange("p (g e t) -> p g e t", e=BUNDLE, t=PACK),
                zb[h][:].rearrange("p t (g e) -> p g e t", e=BUNDLE),
                means[h][:].rearrange("p (g t) -> p g t", t=PACK).unsqueeze(2).broadcast_to([P, groups, BUNDLE, PACK]),
                ALU.subtract,
            )

        cw_rows = ps.tile([P, I], F32, name="cw_rows", tag="zb0")
        for h in range(2):
            nc.tensor.transpose(
                cw_rows[:, HALF * h : HALF * (h + 1)], cw_col[:, h : h + 1].to_broadcast([P, P]), ident[:]
            )

        diffs = sb.tile([P, 2, PACK, HALF], F32, name="diffs", tag="mean1", align_bytes=64)
        ha = [tile(f"ha{h}", [P, HALF * PACK], BF16) for h in range(2)]

        def interleaved(h, first, last):
            return (
                ha[h][:, PACK * first : PACK * last].rearrange("p (c i t) -> p c t i", i=4, t=PACK),
                diffs[:, h, :, first:last].rearrange("p t (c i) -> p c t i", i=4),
            )

        for h in range(2):
            nc.vector.tensor_tensor(diffs[:, h], za[h][:], picked[:, :, HALF * h : HALF * (h + 1)], ALU.subtract)
        nc.scalar.activation(*interleaved(0, 0, HALF), ACT.Relu)
        nc.scalar.activation(*interleaved(1, 0, HALF // 2), ACT.Relu)
        hb_words = tile("hb_words", [P, I], U32)
        hb_plane = tile("hb_plane", [P, I], U8)
        nc.vector.quantize_mx(out=hb_words[:].bitcast(E5M2X4), scales=hb_plane[:], in_=hb[:])
        nc.vector.tensor_scalar_max(*interleaved(1, HALF // 2, HALF), 0.0)

        ha_words = [tile(f"ha_words{h}", [P, HALF], U32) for h in range(2)]
        ha_plane = [tile(f"ha_plane{h}", [P, HALF], U8) for h in range(2)]
        for h in range(2):
            nc.vector.quantize_mx(out=ha_words[h][:].bitcast(E5M2X4), scales=ha_plane[h][:], in_=ha[h][:])

        for h in range(2):
            rows = slice(HALF * h, HALF * (h + 1))
            score = ps.tile([P, I], F32, name=f"score{h}")
            nc.tensor.matmul_mx(
                out=score[:],
                lhsT=ha_words[h][:].bitcast(E5M2X4),
                lhsT_scale=ha_plane[h][:],
                rhs=hb_words[:].bitcast(E5M2X4),
                rhs_scale=hb_plane[:],
                start=True,
                stop=True,
            )
            hinge = tile(f"hinge{h}", [P, I], F32)
            nc.scalar.activation(hinge[:], score[:], ACT.Relu, bias=neg_tg[:, h : h + 1], scale=0.04)
            result = tile(f"result{h}", [P, I], F32)
            nc.vector.tensor_tensor(result[:], hinge[:], cw_rows[:], ALU.mult)
            (nc.sync if h == 0 else nc.scalar).dma_start(out=out[rows, :], in_=result[:])
